import numpy as np
import ml_dtypes


def mxq(x, axis, fmt="e4m3"):
    dtype, down = {"e4m3": (ml_dtypes.float8_e4m3fn, 7), "e5m2": (ml_dtypes.float8_e5m2, 14)}[fmt]
    v = np.moveaxis(np.asarray(x, np.float32).astype(ml_dtypes.bfloat16).astype(np.float64), axis, -1)
    blocks = v.reshape(v.shape[:-1] + (-1, 32))
    amax = np.abs(blocks).max(-1, keepdims=True)
    byte = np.maximum(np.where(amax > 0, np.frexp(amax)[1] - 1 + 127, 0) - down, 1)
    scale = np.exp2(byte - 127.0)
    codes = (blocks / scale).astype(np.float32).astype(dtype).astype(np.float64)
    return np.moveaxis((codes * scale).reshape(v.shape), -1, axis)


WIDE = False


def mx_kscale(k):
    if not WIDE:
        return np.ones(k)
    levels = np.array([10, -10, 5, -5, 0])
    if k % 512:
        return np.exp2(np.random.permutation(np.resize(levels, k // 32))).repeat(32)
    a = np.empty((k // 512, 16))
    for p in range(k // 512):
        a[p, :8] = np.random.permutation(np.resize(levels, 8))
        for g in range(8):
            far = levels[np.abs(levels - a[p, g]) >= 10]
            a[p, g + 8] = far[np.random.randint(len(far))]
    return np.exp2(a.ravel()).repeat(32)


def f64(x):
    return np.asarray(x).astype(np.float64)


def striped(idx):
    return np.tile(idx.reshape(-1, 16).T, (8, 1)).astype(np.uint16)


def unstriped(offs):
    return offs[:16].T.reshape(-1).astype(np.int64)


def pack_weight(w):
    k, n = w.shape
    w = f64(np.asarray(w, np.float32).astype(ml_dtypes.bfloat16)).reshape(k // 32, 32, n)
    amax = np.abs(w).max(1)
    byte = np.clip(np.where(amax > 0, np.frexp(amax)[1] - 1 + 127 - 7, 1), 1, 254)
    scaled = (w * np.exp2(127.0 - byte)[:, None, :]).reshape(k, n).astype(np.float32)
    words = np.ascontiguousarray(scaled.reshape(k // 512, 128, 4, n).transpose(0, 1, 3, 2)).astype(ml_dtypes.float8_e4m3fn).view(np.uint8)
    return words, np.ascontiguousarray(byte.astype(np.uint8).reshape(k // 512, 16, n))


def unpack_weight(words, scales):
    g, p, n, _ = words.shape
    vals = np.ascontiguousarray(words).view(ml_dtypes.float8_e4m3fn).astype(np.float64) * np.repeat(np.exp2(scales.astype(np.float64) - 127.0), 8, axis=1)[..., None]
    return vals.transpose(0, 1, 3, 2).reshape(g * 512, n)


E2M1 = np.array([0.0, 0.5, 1.0, 1.5, 2.0, 3.0, 4.0, 6.0, -0.0, -0.5, -1.0, -1.5, -2.0, -3.0, -4.0, -6.0])


def pack_fp4(w):
    k, n = w.shape
    w = f64(np.asarray(w, np.float32).astype(ml_dtypes.bfloat16)).reshape(k // 32, 32, n)
    amax = np.abs(w).max(1)
    mant, ex = np.frexp(amax / 6.0)
    byte = np.clip(np.where(amax > 0, np.where(mant > 0.5, ex, ex - 1) + 127, 1), 1, 254)
    scaled = (w * np.exp2(127.0 - byte)[:, None, :]).reshape(k, n).astype(np.float32)
    c = np.ascontiguousarray(scaled.reshape(k // 512, 128, 4, n).transpose(0, 1, 3, 2)).astype(ml_dtypes.float4_e2m1fn).view(np.uint8) & 0xF
    words = (c[..., 0::2] | (c[..., 1::2] << 4)).reshape(k // 512, 128, 2 * n)
    return np.ascontiguousarray(words), np.ascontiguousarray(byte.astype(np.uint8).reshape(k // 512, 16, n))


def unpack_fp4(words, scales):
    g, _, n = scales.shape
    words = np.ascontiguousarray(words).reshape(g, 128, n, 2)
    nib = np.empty((g, 128, n, 4), np.uint8)
    nib[..., 0::2] = words & 0xF
    nib[..., 1::2] = words >> 4
    vals = E2M1[nib] * np.repeat(np.exp2(scales.astype(np.float64) - 127.0), 8, axis=1)[..., None]
    return vals.transpose(0, 1, 3, 2).reshape(g * 512, n)


def planes(y):
    n, m = y.shape
    v = y.astype(np.float32).astype(ml_dtypes.bfloat16).astype(np.float64).reshape(n // 32, 32, m)
    top = np.abs(v).max(1)
    byte = np.clip(np.where(top > 0, np.frexp(top)[1] - 1 + 127 - 7, 1), 1, 254)
    codes = (v * np.exp2(127.0 - byte)[:, None, :]).reshape(n, m).astype(np.float32).astype(ml_dtypes.float8_e4m3fn).view(np.uint8)
    words = codes.reshape(n // 512, 128, 4, m).transpose(0, 1, 3, 2)
    return np.ascontiguousarray(words), np.ascontiguousarray(byte.astype(np.uint8).reshape(n // 512, 16, m))


K, T, S, N, H, U = 512, 1024, 512, 512, 512, 1024


def setup_inputs():
    n = np.random.standard_normal
    s = mx_kscale(K)[:, None]
    u = mx_kscale(H)
    packed_xT = pack_weight(n((K, T)) * s)
    packed_w1 = pack_fp4(n((K, N)) / np.sqrt(K) / s)
    packed_w2 = pack_fp4(n((K, N)) / np.sqrt(K) / s)
    packed_w3 = pack_fp4(n((H, N)) / np.sqrt(H) / u[:, None])
    return {
        "x_words": packed_xT[0],
        "x_scales": packed_xT[1],
        "w1_words": packed_w1[0],
        "w1_scales": packed_w1[1],
        "w2_words": packed_w2[0],
        "w2_scales": packed_w2[1],
        "unit": (np.random.uniform(0.6, 1.4, (H, 1)) * u[:, None]).astype(np.float32),
        "w3_words": packed_w3[0],
        "w3_scales": packed_w3[1],
        "offs": striped(np.random.permutation(T)[:S]),
        "b1": striped(np.random.permutation(np.concatenate([np.arange(S), np.random.randint(0, S, U - S)]))),
        "b2": striped(np.random.permutation(np.concatenate([np.arange(S), np.random.randint(0, S, U - S)]))),
        "usr": striped(np.random.permutation(np.concatenate([np.arange(S), np.random.randint(0, S, U - S)]))),
    }


def reference(x_words, x_scales, w1_words, w1_scales, w2_words, w2_scales, unit, w3_words, w3_scales, offs, b1, b2, usr):
    xq = unpack_weight(x_words, x_scales)[:, unstriped(offs)]
    y = unpack_fp4(w1_words, w1_scales).T @ xq
    y_1 = y[:, unstriped(b1)]
    z1 = unpack_fp4(w2_words, w2_scales).T @ xq
    z_2 = z1[:, unstriped(b2)]
    v1_ = y_1 + z_2
    y_2 = y[:, unstriped(b2)]
    z_1 = z1[:, unstriped(b1)]
    v2_ = y_2 + z_1
    adv = v1_ - v2_
    yu = y[:, unstriped(usr)]
    hid = f64(unit) * (adv * yu)
    out_0 = unpack_fp4(w3_words, w3_scales).T @ mxq(hid, 0, "e4m3")
    return (out_0,) + planes(out_0)

@@ -1,0 +1,193 @@
+from contextlib import ExitStack
+
+import concourse.mybir as mybir
+
+K, T, S, N, H, U = 512, 1024, 512, 512, 512, 1024
+FLOPS = 2 * K * N * S * 2 + 2 * H * N * U
+
+F32 = mybir.dt.float32
+BF16 = mybir.dt.bfloat16
+I32 = mybir.dt.int32
+U32 = mybir.dt.uint32
+U16 = mybir.dt.uint16
+U8 = mybir.dt.uint8
+FP8X4 = mybir.dt.float8_e4m3fn_x4
+FP4X4 = mybir.dt.float4_e2m1fn_x4
+MULT = mybir.AluOpType.mult
+SUB = mybir.AluOpType.subtract
+COPY = mybir.ActivationFunctionType.Copy
+
+P = 128
+PACK = 4
+BANK = 512
+CHUNKS = (256, 256, 256, 128, 128)
+
+
+def load_scale_rows(queue, plane, scales):
+    rows = scales[0].bitcast(I32)
+    for q in range(4):
+        queue.dma_start(out=plane[32 * q : 32 * q + 4, :], in_=rows[4 * q : 4 * q + 4, :])
+
+
+def deal_words(engine, dealt, raw):
+    engine.tensor_copy(
+        out=dealt.rearrange("p (t m b) -> p t m b", t=PACK, b=2),
+        in_=raw.bitcast(U8).rearrange("p (m t b) -> p t m b", t=PACK, b=2),
+    )
+
+
+def deal_scales(engine, dealt, raw):
+    engine.tensor_copy(
+        out=dealt.rearrange("p (t m) -> p t m", t=PACK),
+        in_=raw.bitcast(U8).rearrange("p (m t) -> p t m", t=PACK),
+    )
+
+
+def woven(ap):
+    return ap.rearrange("p (c i) t -> p c t i", i=2)
+
+
+def by_pairs(ap):
+    return ap.rearrange("p t (c i) -> p c t i", i=2)
+
+
+def tile_picked_ycompet_adv_po_kernel(
+    tc, x_words, x_scales, w1_words, w1_scales, w2_words, w2_scales, unit, w3_words, w3_scales,
+    offs, b1, b2, usr, out_0, out_1, out_2,
+):
+    nc = tc.nc
+    with ExitStack() as ctx:
+        keep = ctx.enter_context(tc.tile_pool(name="keep", bufs=1))
+        ring = ctx.enter_context(tc.tile_pool(name="ring", bufs=2))
+        psum = ctx.enter_context(tc.psum_pool(name="psum", bufs=1))
+
+        offs_sb = keep.tile([P, S // 16], U16, name="offs_sb")
+        b1_sb = keep.tile([P, U // 16], U16, name="b1_sb")
+        b2_sb = keep.tile([P, U // 16], U16, name="b2_sb")
+        usr_sb = keep.tile([P, U // 16], U16, name="usr_sb")
+        xw = keep.tile([P, T], I32, name="xw", align_bytes=64)
+        xs = keep.tile([P, T // 4], I32, name="xs", align_bytes=64)
+        w_raw = [keep.tile([P, N // 2], I32, name=f"w_raw{a}", align_bytes=64) for a in range(3)]
+        s_raw = [keep.tile([P, N // 4], I32, name=f"s_raw{a}", align_bytes=64) for a in range(3)]
+        unit_sb = keep.tile([P, PACK], F32, name="unit_sb")
+
+        nc.vector.memset(xs[:], 0)
+        nc.gpsimd.memset(s_raw[0][:], 0)
+        nc.vector.memset(s_raw[1][:], 0)
+        nc.gpsimd.memset(s_raw[2][:], 0)
+
+        nc.sync.dma_start(offs_sb[:], offs)
+        nc.sync.dma_start(out=w_raw[0][:], in_=w1_words[0].bitcast(I32))
+        nc.sync.dma_start(out=w_raw[1][:], in_=w2_words[0].bitcast(I32))
+        load_scale_rows(nc.sync, xs, x_scales)
+        nc.sync.dma_start(out=xw[:], in_=x_words[0].rearrange("p n r -> p (n r)").bitcast(I32))
+        load_scale_rows(nc.sync, s_raw[0], w1_scales)
+        load_scale_rows(nc.sync, s_raw[1], w2_scales)
+        nc.sync.dma_start(b2_sb[:], b2)
+        nc.sync.dma_start(out=w_raw[2][:], in_=w3_words[0].bitcast(I32))
+        load_scale_rows(nc.sync, s_raw[2], w3_scales)
+        nc.sync.dma_start(out=unit_sb[:], in_=unit.rearrange("(p t) o -> p (t o)", t=PACK))
+        nc.sync.dma_start(b1_sb[:], b1)
+        nc.sync.dma_start(usr_sb[:], usr)
+
+        w_sb = [keep.tile([P, 2 * N], U8, name=f"w_sb{a}", align_bytes=64) for a in range(3)]
+        s_sb = [keep.tile([P, N], U8, name=f"s_sb{a}", align_bytes=64) for a in range(3)]
+        xq = keep.tile([P, S], I32, name="xq", align_bytes=64)
+        xq_s = keep.tile([P, S], U8, name="xq_s", align_bytes=64)
+
+        deal_words(nc.vector, w_sb[0][:], w_raw[0][:])
+        deal_words(nc.vector, w_sb[1][:], w_raw[1][:])
+        nc.vector.tensor_copy(xq_s[:], xs[:].bitcast(U8).indirect(offs_sb[:]))
+        nc.vector.tensor_copy(xq[:].bitcast(U32), xw[:].bitcast(U32).indirect(offs_sb[:]))
+        deal_scales(nc.vector, s_sb[0][:], s_raw[0][:])
+        deal_scales(nc.vector, s_sb[1][:], s_raw[1][:])
+        deal_words(nc.vector, w_sb[2][:], w_raw[2][:])
+        deal_scales(nc.vector, s_sb[2][:], s_raw[2][:])
+
+        def weights(a, t):
+            return dict(
+                lhsT=w_sb[a][:, 2 * P * t : 2 * P * (t + 1)].bitcast(FP4X4), lhsT_scale=s_sb[a][:, P * t : P * (t + 1)]
+            )
+
+        y_raw = [keep.tile([P, S], F32, name=f"y_raw{t}") for t in range(PACK)]
+        y_unit = [keep.tile([P, S], F32, name=f"y_unit{t}") for t in range(PACK)]
+        diff = [keep.tile([P, S], F32, name=f"diff{t}") for t in range(PACK)]
+        for t in range(PACK):
+            y_ps = psum.tile([P, BANK], F32, name="y_ps", tag=f"bank{2 * t}")
+            z_ps = psum.tile([P, BANK], F32, name="z_ps", tag=f"bank{2 * t + 1}")
+            for a, acc in ((0, y_ps), (1, z_ps)):
+                nc.tensor.matmul_mx(
+                    out=acc[:], rhs=xq[:].bitcast(FP8X4), rhs_scale=xq_s[:], start=True, stop=True, **weights(a, t)
+                )
+            nc.scalar.activation(y_raw[t][:], y_ps[:], COPY)
+            nc.vector.tensor_tensor(diff[t][:], y_raw[t][:], z_ps[:], SUB)
+            nc.vector.tensor_scalar(y_unit[t][:], y_raw[t][:], unit_sb[:, t : t + 1], None, MULT)
+
+        o_codes = keep.tile([P, U], I32, name="o_codes", align_bytes=64)
+        o_scales = keep.tile([P, U], U8, name="o_scales", align_bytes=64)
+        out_rows = out_0.rearrange("(p t) n -> p t n", t=PACK)
+        out_words = out_1[0].rearrange("p n r -> p (n r)").bitcast(I32)
+        starts = [sum(CHUNKS[:c]) for c in range(len(CHUNKS))]
+        held = {}
+
+        def front(c):
+            n, c0 = CHUNKS[c], starts[c]
+            entries = slice(c0 // 16, (c0 + n) // 16)
+            second = ring.tile([P, PACK, n], F32, name="second")
+            adv = ring.tile([P, PACK, n], F32, name="adv")
+            user = ring.tile([P, PACK, n], F32, name="user")
+            hid = ring.tile([P, n, PACK], BF16, name="hid", align_bytes=64)
+            h_codes = ring.tile([P, n], I32, name="h_codes", align_bytes=64)
+            h_scales = ring.tile([P, n], U8, name="h_scales", align_bytes=64)
+            for t in range(PACK):
+                nc.scalar.activation(second[:, t, :], diff[t][:].indirect(b2_sb[:, entries]), COPY)
+                nc.vector.tensor_tensor(adv[:, t, :], diff[t][:].indirect(b1_sb[:, entries]), second[:, t, :], SUB)
+            if c == 0:
+                for t in range(PACK):
+                    nc.vector.tensor_tensor(user[:, t, :], y_unit[t][:].indirect(usr_sb[:, entries]), adv[:, t, :], MULT)
+                nc.vector.tensor_copy(out=woven(hid[:]), in_=by_pairs(user[:]))
+            else:
+                for t in range(PACK):
+                    nc.scalar.activation(user[:, t, :], y_unit[t][:].indirect(usr_sb[:, entries]), COPY)
+                nc.vector.tensor_tensor(woven(hid[:]), by_pairs(adv[:]), by_pairs(user[:]), MULT)
+            nc.vector.quantize_mx(
+                out=h_codes[:].bitcast(FP8X4), scales=h_scales[:], in_=hid[:].rearrange("p n t -> p (n t)")
+            )
+            per_bank = BANK // n
+            banks = []
+            for b in range(PACK // per_bank):
+                acc = psum.tile([P, per_bank, n], F32, name="acc", tag=f"bank{(2 * c + b) % 8}")
+                for j in range(per_bank):
+                    nc.tensor.matmul_mx(
+                        out=acc[:, j, :], rhs=h_codes[:].bitcast(FP8X4), rhs_scale=h_scales[:],
+                        start=True, stop=True, **weights(2, b * per_bank + j),
+                    )
+                banks.append(acc)
+            held[c] = banks
+
+        def back(c):
+            n, c0 = CHUNKS[c], starts[c]
+            per_bank = BANK // n
+            res = ring.tile([P, PACK, n], F32, name="res")
+            rounded = ring.tile([P, n, PACK], BF16, name="rounded", align_bytes=64)
+            for b, acc in enumerate(held[c]):
+                nc.scalar.activation(res[:, b * per_bank : (b + 1) * per_bank, :], acc[:], COPY)
+            nc.sync.dma_start(out=out_rows[:, :, c0 : c0 + n], in_=res[:])
+            nc.vector.tensor_copy(out=woven(rounded[:]), in_=by_pairs(res[:]))
+            nc.vector.quantize_mx(
+                out=o_codes[:, c0 : c0 + n].bitcast(FP8X4),
+                scales=o_scales[:, c0 : c0 + n],
+                in_=rounded[:].rearrange("p n t -> p (n t)"),
+            )
+            nc.sync.dma_start(out=out_words[:, c0 : c0 + n], in_=o_codes[:, c0 : c0 + n])
+
+        for c in range(len(CHUNKS)):
+            front(c)
+            if c > 0:
+                back(c - 1)
+        back(len(CHUNKS) - 1)
+
+        scale_rows = out_2[0].bitcast(I32)
+        for q in range(4):
+            queue = nc.sync if q % 2 == 0 else nc.scalar
+            queue.dma_start(out=scale_rows[4 * q : 4 * q + 4, :], in_=o_scales[32 * q : 32 * q + 4, :].bitcast(I32))

@@ -15,17 +15,28 @@ FP8X4 = mybir.dt.float8_e4m3fn_x4
 FP4X4 = mybir.dt.float4_e2m1fn_x4
 MULT = mybir.AluOpType.mult
 SUB = mybir.AluOpType.subtract
+MIN = mybir.AluOpType.min
+MAX = mybir.AluOpType.max
 COPY = mybir.ActivationFunctionType.Copy
 
 P = 128
 PACK = 4
 BANK = 512
-CHUNKS = (256, 256, 256, 128, 128)
+BIG = 1e38
+CHUNKS = (128, 256, 256, 256, 128)
+PATH = 'VYYYY'
+EVAC = ('VV', 'SS', 'SS', 'SS', 'SV')
+SECOND_TAG = ('s0', 's1', 's0', 's1', 's0')
+ADV_TAG = ('a0', 'a1', 'a2', 'a3', 'a4')
+USER_TAG = ('u0', 'u1', 'codes0', 'codes1', 'codes2')
+ROUND_TAG = ('r0', 'r1', 'r2', 'r3', 'r4')
+LAG = 2
+EARLY = False
 
 
-def load_scale_rows(queue, plane, scales):
+def load_scale_rows(queue, plane, scales, quadrants=range(4)):
     rows = scales[0].bitcast(I32)
-    for q in range(4):
+    for q in quadrants:
         queue.dma_start(out=plane[32 * q : 32 * q + 4, :], in_=rows[4 * q : 4 * q + 4, :])
 
 
@@ -38,8 +49,8 @@ def deal_words(engine, dealt, raw):
 
 def deal_scales(engine, dealt, raw):
     engine.tensor_copy(
-        out=dealt.rearrange("p (t m) -> p t m", t=PACK),
-        in_=raw.bitcast(U8).rearrange("p (m t) -> p t m", t=PACK),
+        out=dealt.rearrange("p (a t m) -> p a t m", t=PACK, m=P),
+        in_=raw.bitcast(U8).rearrange("p (a m t) -> p a t m", t=PACK, m=P),
     )
 
 
@@ -68,48 +79,54 @@ def tile_picked_ycompet_adv_po_kernel(
         xw = keep.tile([P, T], I32, name="xw", align_bytes=64)
         xs = keep.tile([P, T // 4], I32, name="xs", align_bytes=64)
         w_raw = [keep.tile([P, N // 2], I32, name=f"w_raw{a}", align_bytes=64) for a in range(3)]
-        s_raw = [keep.tile([P, N // 4], I32, name=f"s_raw{a}", align_bytes=64) for a in range(3)]
+        s12_raw = keep.tile([P, N // 2], I32, name="s12_raw", tag="scale_rows", align_bytes=64)
+        s3_raw = keep.tile([P, N // 4], I32, name="s3_raw", align_bytes=64)
         unit_sb = keep.tile([P, PACK], F32, name="unit_sb")
 
         nc.vector.memset(xs[:], 0)
-        nc.gpsimd.memset(s_raw[0][:], 0)
-        nc.vector.memset(s_raw[1][:], 0)
-        nc.gpsimd.memset(s_raw[2][:], 0)
+        nc.gpsimd.memset(s12_raw[:], 0)
+        nc.vector.memset(s3_raw[:], 0)
 
+        nc.gpsimd.dma_start(out=w_raw[1][:], in_=w2_words[0].bitcast(I32))
+        nc.gpsimd.dma_start(out=unit_sb[:], in_=unit.rearrange("(p t) o -> p (t o)", t=PACK))
         nc.sync.dma_start(offs_sb[:], offs)
         nc.sync.dma_start(out=w_raw[0][:], in_=w1_words[0].bitcast(I32))
-        nc.sync.dma_start(out=w_raw[1][:], in_=w2_words[0].bitcast(I32))
         load_scale_rows(nc.sync, xs, x_scales)
+        load_scale_rows(nc.sync, s12_raw[:, : N // 4], w1_scales, range(1))
         nc.sync.dma_start(out=xw[:], in_=x_words[0].rearrange("p n r -> p (n r)").bitcast(I32))
-        load_scale_rows(nc.sync, s_raw[0], w1_scales)
-        load_scale_rows(nc.sync, s_raw[1], w2_scales)
+        load_scale_rows(nc.sync, s12_raw[:, : N // 4], w1_scales, range(1, 4))
+        load_scale_rows(nc.sync, s12_raw[:, N // 4 :], w2_scales)
         nc.sync.dma_start(b2_sb[:], b2)
-        nc.sync.dma_start(out=w_raw[2][:], in_=w3_words[0].bitcast(I32))
-        load_scale_rows(nc.sync, s_raw[2], w3_scales)
-        nc.sync.dma_start(out=unit_sb[:], in_=unit.rearrange("(p t) o -> p (t o)", t=PACK))
         nc.sync.dma_start(b1_sb[:], b1)
+        nc.sync.dma_start(out=w_raw[2][:], in_=w3_words[0].bitcast(I32))
+        load_scale_rows(nc.sync, s3_raw, w3_scales)
         nc.sync.dma_start(usr_sb[:], usr)
 
         w_sb = [keep.tile([P, 2 * N], U8, name=f"w_sb{a}", align_bytes=64) for a in range(3)]
-        s_sb = [keep.tile([P, N], U8, name=f"s_sb{a}", align_bytes=64) for a in range(3)]
-        xq = keep.tile([P, S], I32, name="xq", align_bytes=64)
+        s12 = keep.tile([P, 2 * N], U8, name="s12", align_bytes=64)
+        s3 = keep.tile([P, N], U8, name="s3", align_bytes=64)
+        s_sb = [s12[:, :N], s12[:, N:], s3[:]]
+        xq = keep.tile([P, S], I32, name="xq", tag="xq", align_bytes=64)
         xq_s = keep.tile([P, S], U8, name="xq_s", align_bytes=64)
 
         deal_words(nc.vector, w_sb[0][:], w_raw[0][:])
-        deal_words(nc.vector, w_sb[1][:], w_raw[1][:])
+        deal_words(nc.gpsimd, w_sb[1][:], w_raw[1][:])
         nc.vector.tensor_copy(xq_s[:], xs[:].bitcast(U8).indirect(offs_sb[:]))
         nc.vector.tensor_copy(xq[:].bitcast(U32), xw[:].bitcast(U32).indirect(offs_sb[:]))
-        deal_scales(nc.vector, s_sb[0][:], s_raw[0][:])
-        deal_scales(nc.vector, s_sb[1][:], s_raw[1][:])
+        deal_scales(nc.vector, s12[:], s12_raw[:])
         deal_words(nc.vector, w_sb[2][:], w_raw[2][:])
-        deal_scales(nc.vector, s_sb[2][:], s_raw[2][:])
+        deal_scales(nc.vector, s3[:], s3_raw[:])
 
         def weights(a, t):
             return dict(
                 lhsT=w_sb[a][:, 2 * P * t : 2 * P * (t + 1)].bitcast(FP4X4), lhsT_scale=s_sb[a][:, P * t : P * (t + 1)]
             )
 
-        y_raw = [keep.tile([P, S], F32, name=f"y_raw{t}") for t in range(PACK)]
+        inv_raw = keep.tile([P, PACK], F32, name="inv_raw", tag="scale_rows", align_bytes=64)
+        inv_unit = keep.tile([P, PACK], F32, name="inv_unit")
+        nc.vector.reciprocal(inv_raw[:], unit_sb[:])
+        nc.vector.tensor_scalar(inv_unit[:], inv_raw[:], BIG, -BIG, MIN, MAX)
+
         y_unit = [keep.tile([P, S], F32, name=f"y_unit{t}") for t in range(PACK)]
         diff = [keep.tile([P, S], F32, name=f"diff{t}") for t in range(PACK)]
         for t in range(PACK):
@@ -119,9 +136,8 @@ def tile_picked_ycompet_adv_po_kernel(
                 nc.tensor.matmul_mx(
                     out=acc[:], rhs=xq[:].bitcast(FP8X4), rhs_scale=xq_s[:], start=True, stop=True, **weights(a, t)
                 )
-            nc.scalar.activation(y_raw[t][:], y_ps[:], COPY)
-            nc.vector.tensor_tensor(diff[t][:], y_raw[t][:], z_ps[:], SUB)
-            nc.vector.tensor_scalar(y_unit[t][:], y_raw[t][:], unit_sb[:, t : t + 1], None, MULT)
+            nc.scalar.activation(y_unit[t][:], y_ps[:], COPY, scale=unit_sb[:, t : t + 1])
+            nc.vector.scalar_tensor_tensor(diff[t][:], y_unit[t][:], inv_unit[:, t : t + 1], z_ps[:], MULT, SUB)
 
         o_codes = keep.tile([P, U], I32, name="o_codes", align_bytes=64)
         o_scales = keep.tile([P, U], U8, name="o_scales", align_bytes=64)
@@ -129,20 +145,24 @@ def tile_picked_ycompet_adv_po_kernel(
         out_words = out_1[0].rearrange("p n r -> p (n r)").bitcast(I32)
         starts = [sum(CHUNKS[:c]) for c in range(len(CHUNKS))]
         held = {}
+        results = {}
 
         def front(c):
             n, c0 = CHUNKS[c], starts[c]
             entries = slice(c0 // 16, (c0 + n) // 16)
-            second = ring.tile([P, PACK, n], F32, name="second")
-            adv = ring.tile([P, PACK, n], F32, name="adv")
-            user = ring.tile([P, PACK, n], F32, name="user")
-            hid = ring.tile([P, n, PACK], BF16, name="hid", align_bytes=64)
-            h_codes = ring.tile([P, n], I32, name="h_codes", align_bytes=64)
-            h_scales = ring.tile([P, n], U8, name="h_scales", align_bytes=64)
+            second = keep.tile([P, PACK, n], F32, name="second", tag=SECOND_TAG[c], align_bytes=64)
+            adv = keep.tile([P, PACK, n], F32, name="adv", tag=ADV_TAG[c], align_bytes=64)
+            user = keep.tile([P, PACK, n], F32, name="user", tag=USER_TAG[c], align_bytes=64)
+            hid = keep.tile([P, n, PACK], BF16, name="hid", tag=f"hid{c}", align_bytes=64)
+            h_codes = keep.tile([P, n], I32, name="h_codes", tag=f"codes{c}", align_bytes=64)
+            h_scales = keep.tile([P, n], U8, name="h_scales", tag=f"hscales{c}", align_bytes=64)
             for t in range(PACK):
-                nc.scalar.activation(second[:, t, :], diff[t][:].indirect(b2_sb[:, entries]), COPY)
+                if PATH[c] in "YZ":
+                    nc.scalar.activation(second[:, t, :], diff[t][:].indirect(b2_sb[:, entries]), COPY)
+                else:
+                    nc.vector.tensor_copy(second[:, t, :], diff[t][:].indirect(b2_sb[:, entries]))
                 nc.vector.tensor_tensor(adv[:, t, :], diff[t][:].indirect(b1_sb[:, entries]), second[:, t, :], SUB)
-            if c == 0:
+            if PATH[c] in "ZV":
                 for t in range(PACK):
                     nc.vector.tensor_tensor(user[:, t, :], y_unit[t][:].indirect(usr_sb[:, entries]), adv[:, t, :], MULT)
                 nc.vector.tensor_copy(out=woven(hid[:]), in_=by_pairs(user[:]))
@@ -153,27 +173,32 @@ def tile_picked_ycompet_adv_po_kernel(
             nc.vector.quantize_mx(
                 out=h_codes[:].bitcast(FP8X4), scales=h_scales[:], in_=hid[:].rearrange("p n t -> p (n t)")
             )
-            per_bank = BANK // n
             banks = []
-            for b in range(PACK // per_bank):
-                acc = psum.tile([P, per_bank, n], F32, name="acc", tag=f"bank{(2 * c + b) % 8}")
-                for j in range(per_bank):
+            for b in range(2):
+                acc = psum.tile([P, 2, n], F32, name="acc", tag=f"bank{(2 * c + b) % 8}")
+                for j in range(2):
                     nc.tensor.matmul_mx(
                         out=acc[:, j, :], rhs=h_codes[:].bitcast(FP8X4), rhs_scale=h_scales[:],
-                        start=True, stop=True, **weights(2, b * per_bank + j),
+                        start=True, stop=True, **weights(2, 2 * b + j),
                     )
                 banks.append(acc)
             held[c] = banks
 
-        def back(c):
+        def empty(c):
             n, c0 = CHUNKS[c], starts[c]
-            per_bank = BANK // n
-            res = ring.tile([P, PACK, n], F32, name="res")
-            rounded = ring.tile([P, n, PACK], BF16, name="rounded", align_bytes=64)
-            for b, acc in enumerate(held[c]):
-                nc.scalar.activation(res[:, b * per_bank : (b + 1) * per_bank, :], acc[:], COPY)
+            res = keep.tile([P, PACK, n], F32, name="res", tag=f"res{c}", align_bytes=64)
+            for b in range(2):
+                if EVAC[c][b] == "V":
+                    nc.vector.tensor_copy(out=res[:, 2 * b : 2 * b + 2, :], in_=held[c][b][:])
+                else:
+                    nc.scalar.activation(res[:, 2 * b : 2 * b + 2, :], held[c][b][:], COPY)
             nc.sync.dma_start(out=out_rows[:, :, c0 : c0 + n], in_=res[:])
-            nc.vector.tensor_copy(out=woven(rounded[:]), in_=by_pairs(res[:]))
+            results[c] = res
+
+        def finish(c):
+            n, c0 = CHUNKS[c], starts[c]
+            rounded = keep.tile([P, n, PACK], BF16, name="rounded", tag=ROUND_TAG[c], align_bytes=64)
+            nc.vector.tensor_copy(out=woven(rounded[:]), in_=by_pairs(results[c][:]))
             nc.vector.quantize_mx(
                 out=o_codes[:, c0 : c0 + n].bitcast(FP8X4),
                 scales=o_scales[:, c0 : c0 + n],
@@ -181,11 +206,16 @@ def tile_picked_ycompet_adv_po_kernel(
             )
             nc.sync.dma_start(out=out_words[:, c0 : c0 + n], in_=o_codes[:, c0 : c0 + n])
 
-        for c in range(len(CHUNKS)):
-            front(c)
-            if c > 0:
-                back(c - 1)
-        back(len(CHUNKS) - 1)
+        last = len(CHUNKS) - 1
+        for c in range(last + 1 + LAG):
+            if 0 <= c - 1 <= last and EARLY:
+                empty(c - 1)
+            if c <= last:
+                front(c)
+            if 0 <= c - 1 <= last and not EARLY:
+                empty(c - 1)
+            if 0 <= c - LAG <= last:
+                finish(c - LAG)
 
         scale_rows = out_2[0].bitcast(I32)
         for q in range(4):

@@ -23,15 +23,16 @@ P = 128
 PACK = 4
 BANK = 512
 BIG = 1e38
-CHUNKS = (128, 256, 256, 256, 128)
-PATH = 'VYYYY'
-EVAC = ('VV', 'SS', 'SS', 'SS', 'SV')
+CHUNKS = (256, 256, 256, 128, 128)
+PATH = 'WYYYY'
+EVAC = ('SS', 'SS', 'SS', 'SS', 'SV')
 SECOND_TAG = ('s0', 's1', 's0', 's1', 's0')
 ADV_TAG = ('a0', 'a1', 'a2', 'a3', 'a4')
-USER_TAG = ('u0', 'u1', 'codes0', 'codes1', 'codes2')
+USER_TAG = ('u0', 'u1', 'hid0', 'hid1', 'hid2')
 ROUND_TAG = ('r0', 'r1', 'r2', 'r3', 'r4')
-LAG = 2
-EARLY = False
+LAG = 3
+EARLY = 2
+WORDS = (0, 2, 4)
 
 
 def load_scale_rows(queue, plane, scales, quadrants=range(4)):
@@ -204,16 +205,21 @@ def tile_picked_ycompet_adv_po_kernel(
                 scales=o_scales[:, c0 : c0 + n],
                 in_=rounded[:].rearrange("p n t -> p (n t)"),
             )
-            nc.sync.dma_start(out=out_words[:, c0 : c0 + n], in_=o_codes[:, c0 : c0 + n])
+            if c in WORDS:
+                w0 = starts[max([k + 1 for k in WORDS if k < c] + [0])]
+                nc.sync.dma_start(out=out_words[:, w0 : c0 + n], in_=o_codes[:, w0 : c0 + n])
 
         last = len(CHUNKS) - 1
         for c in range(last + 1 + LAG):
-            if 0 <= c - 1 <= last and EARLY:
-                empty(c - 1)
             if c <= last:
                 front(c)
-            if 0 <= c - 1 <= last and not EARLY:
+            if 0 <= c - 1 <= last and c - 1 < EARLY:
                 empty(c - 1)
+            if c == last:
+                for e in range(EARLY, last):
+                    empty(e)
+            if c == last + 1 and EARLY <= last:
+                empty(last)
             if 0 <= c - LAG <= last:
                 finish(c - LAG)
 

from contextlib import ExitStack

import concourse.mybir as mybir

K, T, S, N, H, U = 512, 1024, 512, 512, 512, 1024
FLOPS = 2 * K * N * S * 2 + 2 * H * N * U

F32 = mybir.dt.float32
BF16 = mybir.dt.bfloat16
I32 = mybir.dt.int32
U32 = mybir.dt.uint32
U16 = mybir.dt.uint16
U8 = mybir.dt.uint8
FP8X4 = mybir.dt.float8_e4m3fn_x4
FP4X4 = mybir.dt.float4_e2m1fn_x4
MULT = mybir.AluOpType.mult
SUB = mybir.AluOpType.subtract
MIN = mybir.AluOpType.min
MAX = mybir.AluOpType.max
COPY = mybir.ActivationFunctionType.Copy

P = 128
PACK = 4
BANK = 512
BIG = 1e38
CHUNKS = (256, 256, 256, 128, 128)
PATH = 'WYYYY'
EVAC = ('SS', 'SS', 'SS', 'SS', 'SV')
SECOND_TAG = ('s0', 's1', 's0', 's1', 's0')
ADV_TAG = ('a0', 'a1', 'a2', 'a3', 'a4')
USER_TAG = ('u0', 'u1', 'hid0', 'hid1', 'hid2')
ROUND_TAG = ('r0', 'r1', 'r2', 'r3', 'r4')
LAG = 3
EARLY = 2
WORDS = (0, 2, 4)


def load_scale_rows(queue, plane, scales, quadrants=range(4)):
    rows = scales[0].bitcast(I32)
    for q in quadrants:
        queue.dma_start(out=plane[32 * q : 32 * q + 4, :], in_=rows[4 * q : 4 * q + 4, :])


def deal_words(engine, dealt, raw):
    engine.tensor_copy(
        out=dealt.rearrange("p (t m b) -> p t m b", t=PACK, b=2),
        in_=raw.bitcast(U8).rearrange("p (m t b) -> p t m b", t=PACK, b=2),
    )


def deal_scales(engine, dealt, raw):
    engine.tensor_copy(
        out=dealt.rearrange("p (a t m) -> p a t m", t=PACK, m=P),
        in_=raw.bitcast(U8).rearrange("p (a m t) -> p a t m", t=PACK, m=P),
    )


def woven(ap):
    return ap.rearrange("p (c i) t -> p c t i", i=2)


def by_pairs(ap):
    return ap.rearrange("p t (c i) -> p c t i", i=2)


def tile_picked_ycompet_adv_po_kernel(
    tc, x_words, x_scales, w1_words, w1_scales, w2_words, w2_scales, unit, w3_words, w3_scales,
    offs, b1, b2, usr, out_0, out_1, out_2,
):
    nc = tc.nc
    with ExitStack() as ctx:
        keep = ctx.enter_context(tc.tile_pool(name="keep", bufs=1))
        ring = ctx.enter_context(tc.tile_pool(name="ring", bufs=2))
        psum = ctx.enter_context(tc.psum_pool(name="psum", bufs=1))

        offs_sb = keep.tile([P, S // 16], U16, name="offs_sb")
        b1_sb = keep.tile([P, U // 16], U16, name="b1_sb")
        b2_sb = keep.tile([P, U // 16], U16, name="b2_sb")
        usr_sb = keep.tile([P, U // 16], U16, name="usr_sb")
        xw = keep.tile([P, T], I32, name="xw", align_bytes=64)
        xs = keep.tile([P, T // 4], I32, name="xs", align_bytes=64)
        w_raw = [keep.tile([P, N // 2], I32, name=f"w_raw{a}", align_bytes=64) for a in range(3)]
        s12_raw = keep.tile([P, N // 2], I32, name="s12_raw", tag="scale_rows", align_bytes=64)
        s3_raw = keep.tile([P, N // 4], I32, name="s3_raw", align_bytes=64)
        unit_sb = keep.tile([P, PACK], F32, name="unit_sb")

        nc.vector.memset(xs[:], 0)
        nc.gpsimd.memset(s12_raw[:], 0)
        nc.vector.memset(s3_raw[:], 0)

        nc.gpsimd.dma_start(out=w_raw[1][:], in_=w2_words[0].bitcast(I32))
        nc.gpsimd.dma_start(out=unit_sb[:], in_=unit.rearrange("(p t) o -> p (t o)", t=PACK))
        nc.sync.dma_start(offs_sb[:], offs)
        nc.sync.dma_start(out=w_raw[0][:], in_=w1_words[0].bitcast(I32))
        load_scale_rows(nc.sync, xs, x_scales)
        load_scale_rows(nc.sync, s12_raw[:, : N // 4], w1_scales, range(1))
        nc.sync.dma_start(out=xw[:], in_=x_words[0].rearrange("p n r -> p (n r)").bitcast(I32))
        load_scale_rows(nc.sync, s12_raw[:, : N // 4], w1_scales, range(1, 4))
        load_scale_rows(nc.sync, s12_raw[:, N // 4 :], w2_scales)
        nc.sync.dma_start(b2_sb[:], b2)
        nc.sync.dma_start(b1_sb[:], b1)
        nc.sync.dma_start(out=w_raw[2][:], in_=w3_words[0].bitcast(I32))
        load_scale_rows(nc.sync, s3_raw, w3_scales)
        nc.sync.dma_start(usr_sb[:], usr)

        w_sb = [keep.tile([P, 2 * N], U8, name=f"w_sb{a}", align_bytes=64) for a in range(3)]
        s12 = keep.tile([P, 2 * N], U8, name="s12", align_bytes=64)
        s3 = keep.tile([P, N], U8, name="s3", align_bytes=64)
        s_sb = [s12[:, :N], s12[:, N:], s3[:]]
        xq = keep.tile([P, S], I32, name="xq", tag="xq", align_bytes=64)
        xq_s = keep.tile([P, S], U8, name="xq_s", align_bytes=64)

        deal_words(nc.vector, w_sb[0][:], w_raw[0][:])
        deal_words(nc.gpsimd, w_sb[1][:], w_raw[1][:])
        nc.vector.tensor_copy(xq_s[:], xs[:].bitcast(U8).indirect(offs_sb[:]))
        nc.vector.tensor_copy(xq[:].bitcast(U32), xw[:].bitcast(U32).indirect(offs_sb[:]))
        deal_scales(nc.vector, s12[:], s12_raw[:])
        deal_words(nc.vector, w_sb[2][:], w_raw[2][:])
        deal_scales(nc.vector, s3[:], s3_raw[:])

        def weights(a, t):
            return dict(
                lhsT=w_sb[a][:, 2 * P * t : 2 * P * (t + 1)].bitcast(FP4X4), lhsT_scale=s_sb[a][:, P * t : P * (t + 1)]
            )

        inv_raw = keep.tile([P, PACK], F32, name="inv_raw", tag="scale_rows", align_bytes=64)
        inv_unit = keep.tile([P, PACK], F32, name="inv_unit")
        nc.vector.reciprocal(inv_raw[:], unit_sb[:])
        nc.vector.tensor_scalar(inv_unit[:], inv_raw[:], BIG, -BIG, MIN, MAX)

        y_unit = [keep.tile([P, S], F32, name=f"y_unit{t}") for t in range(PACK)]
        diff = [keep.tile([P, S], F32, name=f"diff{t}") for t in range(PACK)]
        for t in range(PACK):
            y_ps = psum.tile([P, BANK], F32, name="y_ps", tag=f"bank{2 * t}")
            z_ps = psum.tile([P, BANK], F32, name="z_ps", tag=f"bank{2 * t + 1}")
            for a, acc in ((0, y_ps), (1, z_ps)):
                nc.tensor.matmul_mx(
                    out=acc[:], rhs=xq[:].bitcast(FP8X4), rhs_scale=xq_s[:], start=True, stop=True, **weights(a, t)
                )
            nc.scalar.activation(y_unit[t][:], y_ps[:], COPY, scale=unit_sb[:, t : t + 1])
            nc.vector.scalar_tensor_tensor(diff[t][:], y_unit[t][:], inv_unit[:, t : t + 1], z_ps[:], MULT, SUB)

        o_codes = keep.tile([P, U], I32, name="o_codes", align_bytes=64)
        o_scales = keep.tile([P, U], U8, name="o_scales", align_bytes=64)
        out_rows = out_0.rearrange("(p t) n -> p t n", t=PACK)
        out_words = out_1[0].rearrange("p n r -> p (n r)").bitcast(I32)
        starts = [sum(CHUNKS[:c]) for c in range(len(CHUNKS))]
        held = {}
        results = {}

        def front(c):
            n, c0 = CHUNKS[c], starts[c]
            entries = slice(c0 // 16, (c0 + n) // 16)
            second = keep.tile([P, PACK, n], F32, name="second", tag=SECOND_TAG[c], align_bytes=64)
            adv = keep.tile([P, PACK, n], F32, name="adv", tag=ADV_TAG[c], align_bytes=64)
            user = keep.tile([P, PACK, n], F32, name="user", tag=USER_TAG[c], align_bytes=64)
            hid = keep.tile([P, n, PACK], BF16, name="hid", tag=f"hid{c}", align_bytes=64)
            h_codes = keep.tile([P, n], I32, name="h_codes", tag=f"codes{c}", align_bytes=64)
            h_scales = keep.tile([P, n], U8, name="h_scales", tag=f"hscales{c}", align_bytes=64)
            for t in range(PACK):
                if PATH[c] in "YZ":
                    nc.scalar.activation(second[:, t, :], diff[t][:].indirect(b2_sb[:, entries]), COPY)
                else:
                    nc.vector.tensor_copy(second[:, t, :], diff[t][:].indirect(b2_sb[:, entries]))
                nc.vector.tensor_tensor(adv[:, t, :], diff[t][:].indirect(b1_sb[:, entries]), second[:, t, :], SUB)
            if PATH[c] in "ZV":
                for t in range(PACK):
                    nc.vector.tensor_tensor(user[:, t, :], y_unit[t][:].indirect(usr_sb[:, entries]), adv[:, t, :], MULT)
                nc.vector.tensor_copy(out=woven(hid[:]), in_=by_pairs(user[:]))
            else:
                for t in range(PACK):
                    nc.scalar.activation(user[:, t, :], y_unit[t][:].indirect(usr_sb[:, entries]), COPY)
                nc.vector.tensor_tensor(woven(hid[:]), by_pairs(adv[:]), by_pairs(user[:]), MULT)
            nc.vector.quantize_mx(
                out=h_codes[:].bitcast(FP8X4), scales=h_scales[:], in_=hid[:].rearrange("p n t -> p (n t)")
            )
            banks = []
            for b in range(2):
                acc = psum.tile([P, 2, n], F32, name="acc", tag=f"bank{(2 * c + b) % 8}")
                for j in range(2):
                    nc.tensor.matmul_mx(
                        out=acc[:, j, :], rhs=h_codes[:].bitcast(FP8X4), rhs_scale=h_scales[:],
                        start=True, stop=True, **weights(2, 2 * b + j),
                    )
                banks.append(acc)
            held[c] = banks

        def empty(c):
            n, c0 = CHUNKS[c], starts[c]
            res = keep.tile([P, PACK, n], F32, name="res", tag=f"res{c}", align_bytes=64)
            for b in range(2):
                if EVAC[c][b] == "V":
                    nc.vector.tensor_copy(out=res[:, 2 * b : 2 * b + 2, :], in_=held[c][b][:])
                else:
                    nc.scalar.activation(res[:, 2 * b : 2 * b + 2, :], held[c][b][:], COPY)
            nc.sync.dma_start(out=out_rows[:, :, c0 : c0 + n], in_=res[:])
            results[c] = res

        def finish(c):
            n, c0 = CHUNKS[c], starts[c]
            rounded = keep.tile([P, n, PACK], BF16, name="rounded", tag=ROUND_TAG[c], align_bytes=64)
            nc.vector.tensor_copy(out=woven(rounded[:]), in_=by_pairs(results[c][:]))
            nc.vector.quantize_mx(
                out=o_codes[:, c0 : c0 + n].bitcast(FP8X4),
                scales=o_scales[:, c0 : c0 + n],
                in_=rounded[:].rearrange("p n t -> p (n t)"),
            )
            if c in WORDS:
                w0 = starts[max([k + 1 for k in WORDS if k < c] + [0])]
                nc.sync.dma_start(out=out_words[:, w0 : c0 + n], in_=o_codes[:, w0 : c0 + n])

        last = len(CHUNKS) - 1
        for c in range(last + 1 + LAG):
            if c <= last:
                front(c)
            if 0 <= c - 1 <= last and c - 1 < EARLY:
                empty(c - 1)
            if c == last:
                for e in range(EARLY, last):
                    empty(e)
            if c == last + 1 and EARLY <= last:
                empty(last)
            if 0 <= c - LAG <= last:
                finish(c - LAG)

        scale_rows = out_2[0].bitcast(I32)
        for q in range(4):
            queue = nc.sync if q % 2 == 0 else nc.scalar
            queue.dma_start(out=scale_rows[4 * q : 4 * q + 4, :], in_=o_scales[32 * q : 32 * q + 4, :].bitcast(I32))
